import numpy as np, ml_dtypes
CORES = [40,41,42,43,44,45,46,47,208,209,210,211,212,213,214,215]
N = 16
def setup_inputs(rng):
    return {"x": rng.standard_normal((N, 128, 2048), dtype=np.float32).astype(ml_dtypes.bfloat16)}
def reference(x):
    s = x.max(axis=0)
    return {"y": np.broadcast_to(s, (N,) + s.shape)}

@@ -1,0 +1,78 @@
+from concourse.bass import DstId, RemoteDMATransfer
+
+SCRATCH = {
+    "xs": ("dram", [8, 128, 256], "bfloat16"),
+    "land": ("dram", [14, 128, 256], "bfloat16"),
+    "rl": ("dram", [4, 128, 256], "bfloat16"),
+    "fin": ("dram", [8, 128, 256], "bfloat16"),
+}
+SEMAPHORES = ["ld", "sc", "rr", "fa", "snt", "st"]
+
+OWNERS = (2, 3, 6, 7)
+PAIR = ((0, 3), (1, 2), (4, 7), (5, 6))
+MAX = 2
+
+
+def rank_program(g, core, T, topo):
+    if T.rank_of(core) is None:
+        return
+    k = core % 8
+    base = core - k
+    other = [b for b in (T.cores[0], T.cores[8]) if b != base][0]
+    sem = T.sem
+
+    def did(dst):
+        rid, pid = topo.addr(dst, core)
+        return DstId(rid=rid, pnc=pid)
+
+    sent = 0
+    g.sync.dma_start(T.xs[:], T.x[:]).then_inc(sem.ld, 16)
+    g.wait_ge(sem.ld, 16)
+
+    trs = []
+    eng = 0
+    for q, h in enumerate(OWNERS):
+        if h == k:
+            continue
+        idx = k if k < h else k - 1
+        for j in range(2):
+            trs.append(RemoteDMATransfer(dst_ids=[did(base + h)], dma_engine_mask=3 << eng, remote_sem=sem.sc,
+                                         src=T.xs[2 * q + j], dst=T.land[2 * idx + j], alu_op=0))
+            eng += 2
+            sent += 2
+    g.remote_dma_fused(trs, local_sem=sem.snt)
+
+    if k in OWNERS:
+        q = OWNERS.index(k)
+        u, v = PAIR[q]
+        g.wait_ge(sem.sc, 7 * 2 * 2)
+        trs = []
+        for j in range(2):
+            srcs = [T.land[2 * i + j] for i in range(7)] + [T.xs[2 * q + j]]
+            trs.append(RemoteDMATransfer(dst_ids=[did(other + u), did(other + v)], dma_engine_mask=0xF << (4 * j),
+                                         remote_sem=sem.rr, srcs=srcs, dsts=[T.rl[2 + j], T.rl[2 + j]], alu_op=MAX))
+            trs.append(RemoteDMATransfer(dst_ids=[did(base + u), did(base + v)], dma_engine_mask=0xF00 << (4 * j),
+                                         remote_sem=sem.rr, srcs=srcs, dsts=[T.rl[j], T.rl[j]], alu_op=MAX))
+            sent += 8
+        g.remote_dma_fused(trs, local_sem=sem.snt)
+
+    q = [i for i, p in enumerate(PAIR) if k in p][0]
+    j = PAIR[q].index(k)
+    partner = PAIR[q][1 - j]
+    mine, his = 2 * q + j, 2 * q + 1 - j
+    g.wait_ge(sem.rr, 16)
+    others = [(k + 1 + i) % 8 for i in range(7)]
+    trs = []
+    for lo, hi, mask in ((0, 4, 0x00FF), (4, 6, 0x0F00), (6, 7, 0x3000)):
+        ds = others[lo:hi]
+        trs.append(RemoteDMATransfer(dst_ids=[did(base + d) for d in ds], dma_engine_mask=mask, remote_sem=sem.fa,
+                                     srcs=[T.rl[j], T.rl[2 + j]], dsts=[T.fin[mine] for d in ds], alu_op=MAX))
+    trs.append(RemoteDMATransfer(dst_ids=[did(base + partner)], dma_engine_mask=0xC000, remote_sem=sem.fa,
+                                 srcs=[T.rl[1 - j], T.rl[3 - j]], dsts=[T.fin[his]], alu_op=MAX))
+    sent += 16
+    g.remote_dma_fused(trs, local_sem=sem.snt)
+
+    g.sync.wait_ge(sem.fa, 4 * 8 + 2 * 4 + 2 + 2)
+    g.sync.dma_start(T.y[:], T.fin[:]).then_inc(sem.st, 16)
+    g.sync.wait_ge(sem.st, 16)
+    g.wait_ge(sem.snt, sent)

@@ -1,12 +1,14 @@
 from concourse.bass import DstId, RemoteDMATransfer
 
+S = 2
+W = 256 // S
 SCRATCH = {
-    "xs": ("dram", [8, 128, 256], "bfloat16"),
-    "land": ("dram", [14, 128, 256], "bfloat16"),
-    "rl": ("dram", [4, 128, 256], "bfloat16"),
-    "fin": ("dram", [8, 128, 256], "bfloat16"),
+    "xs": ("dram", [8 * S, 128, W], "bfloat16"),
+    "land": ("dram", [14 * S, 128, W], "bfloat16"),
+    "rl": ("dram", [4 * S, 128, W], "bfloat16"),
+    "fin": ("dram", [8 * S, 128, W], "bfloat16"),
 }
-SEMAPHORES = ["ld", "sc", "rr", "fa", "snt", "st"]
+SEMAPHORES = ["snt", "st"] + ["%s%d" % (n, t) for n in ("ld", "sc", "rr", "fa") for t in range(S)]
 
 OWNERS = (2, 3, 6, 7)
 PAIR = ((0, 3), (1, 2), (4, 7), (5, 6))
@@ -20,59 +22,68 @@ def rank_program(g, core, T, topo):
     base = core - k
     other = [b for b in (T.cores[0], T.cores[8]) if b != base][0]
     sem = T.sem
+    R = 128 // S
+    sent = [0]
 
     def did(dst):
         rid, pid = topo.addr(dst, core)
         return DstId(rid=rid, pnc=pid)
 
-    sent = 0
-    g.sync.dma_start(T.xs[:], T.x[:]).then_inc(sem.ld, 16)
-    g.wait_ge(sem.ld, 16)
+    for t in range(S):
+        g.sync.dma_start(T.xs[8 * t:8 * t + 8], T.x[R * t:R * t + R, :]).then_inc(sem["ld%d" % t], 16)
 
-    trs = []
-    eng = 0
-    for q, h in enumerate(OWNERS):
-        if h == k:
-            continue
-        idx = k if k < h else k - 1
-        for j in range(2):
-            trs.append(RemoteDMATransfer(dst_ids=[did(base + h)], dma_engine_mask=3 << eng, remote_sem=sem.sc,
-                                         src=T.xs[2 * q + j], dst=T.land[2 * idx + j], alu_op=0))
-            eng += 2
-            sent += 2
-    g.remote_dma_fused(trs, local_sem=sem.snt)
+    for t in range(S):
+        g.wait_ge(sem["ld%d" % t], 16)
+        trs = []
+        eng = 0
+        for q, h in enumerate(OWNERS):
+            if h == k:
+                continue
+            idx = k if k < h else k - 1
+            for j in range(2):
+                trs.append(RemoteDMATransfer(dst_ids=[did(base + h)], dma_engine_mask=3 << eng,
+                                             remote_sem=sem["sc%d" % t], src=T.xs[8 * t + 2 * q + j],
+                                             dst=T.land[14 * t + 2 * idx + j], alu_op=0))
+                eng += 2
+                sent[0] += 2
+        g.remote_dma_fused(trs, local_sem=sem.snt)
 
     if k in OWNERS:
         q = OWNERS.index(k)
         u, v = PAIR[q]
-        g.wait_ge(sem.sc, 7 * 2 * 2)
-        trs = []
-        for j in range(2):
-            srcs = [T.land[2 * i + j] for i in range(7)] + [T.xs[2 * q + j]]
-            trs.append(RemoteDMATransfer(dst_ids=[did(other + u), did(other + v)], dma_engine_mask=0xF << (4 * j),
-                                         remote_sem=sem.rr, srcs=srcs, dsts=[T.rl[2 + j], T.rl[2 + j]], alu_op=MAX))
-            trs.append(RemoteDMATransfer(dst_ids=[did(base + u), did(base + v)], dma_engine_mask=0xF00 << (4 * j),
-                                         remote_sem=sem.rr, srcs=srcs, dsts=[T.rl[j], T.rl[j]], alu_op=MAX))
-            sent += 8
-        g.remote_dma_fused(trs, local_sem=sem.snt)
+        for t in range(S):
+            g.wait_ge(sem["sc%d" % t], 7 * 2 * 2)
+            trs = []
+            for j in range(2):
+                srcs = [T.land[14 * t + 2 * i + j] for i in range(7)] + [T.xs[8 * t + 2 * q + j]]
+                far, near = T.rl[4 * t + 2 + j], T.rl[4 * t + j]
+                trs.append(RemoteDMATransfer(dst_ids=[did(other + u), did(other + v)], dma_engine_mask=0xF << (4 * j),
+                                             remote_sem=sem["rr%d" % t], srcs=srcs, dsts=[far, far], alu_op=MAX))
+                trs.append(RemoteDMATransfer(dst_ids=[did(base + u), did(base + v)], dma_engine_mask=0xF00 << (4 * j),
+                                             remote_sem=sem["rr%d" % t], srcs=srcs, dsts=[near, near], alu_op=MAX))
+                sent[0] += 8
+            g.remote_dma_fused(trs, local_sem=sem.snt)
 
     q = [i for i, p in enumerate(PAIR) if k in p][0]
     j = PAIR[q].index(k)
     partner = PAIR[q][1 - j]
-    mine, his = 2 * q + j, 2 * q + 1 - j
-    g.wait_ge(sem.rr, 16)
     others = [(k + 1 + i) % 8 for i in range(7)]
-    trs = []
-    for lo, hi, mask in ((0, 4, 0x00FF), (4, 6, 0x0F00), (6, 7, 0x3000)):
-        ds = others[lo:hi]
-        trs.append(RemoteDMATransfer(dst_ids=[did(base + d) for d in ds], dma_engine_mask=mask, remote_sem=sem.fa,
-                                     srcs=[T.rl[j], T.rl[2 + j]], dsts=[T.fin[mine] for d in ds], alu_op=MAX))
-    trs.append(RemoteDMATransfer(dst_ids=[did(base + partner)], dma_engine_mask=0xC000, remote_sem=sem.fa,
-                                 srcs=[T.rl[1 - j], T.rl[3 - j]], dsts=[T.fin[his]], alu_op=MAX))
-    sent += 16
-    g.remote_dma_fused(trs, local_sem=sem.snt)
+    for t in range(S):
+        mine, his = 8 * t + 2 * q + j, 8 * t + 2 * q + 1 - j
+        g.wait_ge(sem["rr%d" % t], 16)
+        trs = []
+        for lo, hi, mask in ((0, 4, 0x00FF), (4, 6, 0x0F00), (6, 7, 0x3000)):
+            ds = others[lo:hi]
+            trs.append(RemoteDMATransfer(dst_ids=[did(base + d) for d in ds], dma_engine_mask=mask,
+                                         remote_sem=sem["fa%d" % t], srcs=[T.rl[4 * t + j], T.rl[4 * t + 2 + j]],
+                                         dsts=[T.fin[mine] for d in ds], alu_op=MAX))
+        trs.append(RemoteDMATransfer(dst_ids=[did(base + partner)], dma_engine_mask=0xC000, remote_sem=sem["fa%d" % t],
+                                     srcs=[T.rl[4 * t + 1 - j], T.rl[4 * t + 3 - j]], dsts=[T.fin[his]], alu_op=MAX))
+        sent[0] += 16
+        g.remote_dma_fused(trs, local_sem=sem.snt)
 
-    g.sync.wait_ge(sem.fa, 4 * 8 + 2 * 4 + 2 + 2)
-    g.sync.dma_start(T.y[:], T.fin[:]).then_inc(sem.st, 16)
-    g.sync.wait_ge(sem.st, 16)
-    g.wait_ge(sem.snt, sent)
+    for t in range(S):
+        g.sync.wait_ge(sem["fa%d" % t], 4 * 8 + 2 * 4 + 2 + 2)
+        g.sync.dma_start(T.y[R * t:R * t + R, :], T.fin[8 * t:8 * t + 8]).then_inc(sem.st, 16)
+    g.sync.wait_ge(sem.st, 16 * S)
+    g.wait_ge(sem.snt, sent[0])

@@ -4,24 +4,16 @@ S = 2
 W = 256 // S
 SCRATCH = {
     "xs": ("dram", [8 * S, 128, W], "bfloat16"),
-    "land": ("dram", [14 * S, 128, W], "bfloat16"),
-    "rl": ("dram", [4 * S, 128, W], "bfloat16"),
+    "land": ("dram", [7 * S, 128, W], "bfloat16"),
     "fin": ("dram", [8 * S, 128, W], "bfloat16"),
 }
-SEMAPHORES = ["snt", "st"] + ["%s%d" % (n, t) for n in ("ld", "sc", "rr", "fa") for t in range(S)]
-
-OWNERS = (2, 3, 6, 7)
-PAIR = ((0, 3), (1, 2), (4, 7), (5, 6))
+SEMAPHORES = ["snt", "st"] + ["%s%d" % (n, t) for n in ("ld", "sc", "hp", "fr", "ag") for t in range(S)]
 MAX = 2
 
 
 def rank_program(g, core, T, topo):
-    if T.rank_of(core) is None:
-        return
-    k = core % 8
-    base = core - k
-    other = [b for b in (T.cores[0], T.cores[8]) if b != base][0]
     sem = T.sem
+    bases = (T.cores[0], T.cores[8])
     R = 128 // S
     sent = [0]
 
@@ -29,61 +21,66 @@ def rank_program(g, core, T, topo):
         rid, pid = topo.addr(dst, core)
         return DstId(rid=rid, pnc=pid)
 
+    def owner(e, side):
+        return bases[side] + (e ^ 2 if side else e)
+
+    def helper(e):
+        return (bases[0] ^ 8) + e if e & 2 else (bases[1] ^ 8) + (e | 2)
+
+    if T.rank_of(core) is None:
+        for e in range(8):
+            if helper(e) == core:
+                for t in range(S):
+                    g.wait_ge(sem["hp%d" % t], 16)
+                    g.remote_dma_fused([RemoteDMATransfer(
+                        dst_ids=[did(owner(e, 0)), did(owner(e, 1))], dma_engine_mask=0xFF, remote_sem=sem["fr%d" % t],
+                        srcs=[T.land[2 * t], T.land[2 * t + 1]], dsts=[T.fin[8 * t + e], T.fin[8 * t + e]],
+                        alu_op=MAX)], local_sem=sem.snt)
+                g.wait_ge(sem.snt, 8 * S)
+        return
+
+    k = core % 8
+    base = core - k
+    side = bases.index(base)
+    mine = k ^ 2 if side else k
+    others = [d for d in range(8) if d != k]
+
     for t in range(S):
         g.sync.dma_start(T.xs[8 * t:8 * t + 8], T.x[R * t:R * t + R, :]).then_inc(sem["ld%d" % t], 16)
 
     for t in range(S):
         g.wait_ge(sem["ld%d" % t], 16)
         trs = []
-        eng = 0
-        for q, h in enumerate(OWNERS):
-            if h == k:
-                continue
-            idx = k if k < h else k - 1
-            for j in range(2):
-                trs.append(RemoteDMATransfer(dst_ids=[did(base + h)], dma_engine_mask=3 << eng,
-                                             remote_sem=sem["sc%d" % t], src=T.xs[8 * t + 2 * q + j],
-                                             dst=T.land[14 * t + 2 * idx + j], alu_op=0))
-                eng += 2
-                sent[0] += 2
+        for i, d in enumerate(others):
+            e = d ^ 2 if side else d
+            idx = k if k < d else k - 1
+            trs.append(RemoteDMATransfer(dst_ids=[did(base + d)], dma_engine_mask=3 << (2 + 2 * i),
+                                         remote_sem=sem["sc%d" % t], src=T.xs[8 * t + e], dst=T.land[7 * t + idx],
+                                         alu_op=0))
+            sent[0] += 2
         g.remote_dma_fused(trs, local_sem=sem.snt)
 
-    if k in OWNERS:
-        q = OWNERS.index(k)
-        u, v = PAIR[q]
-        for t in range(S):
-            g.wait_ge(sem["sc%d" % t], 7 * 2 * 2)
-            trs = []
-            for j in range(2):
-                srcs = [T.land[14 * t + 2 * i + j] for i in range(7)] + [T.xs[8 * t + 2 * q + j]]
-                far, near = T.rl[4 * t + 2 + j], T.rl[4 * t + j]
-                trs.append(RemoteDMATransfer(dst_ids=[did(other + u), did(other + v)], dma_engine_mask=0xF << (4 * j),
-                                             remote_sem=sem["rr%d" % t], srcs=srcs, dsts=[far, far], alu_op=MAX))
-                trs.append(RemoteDMATransfer(dst_ids=[did(base + u), did(base + v)], dma_engine_mask=0xF00 << (4 * j),
-                                             remote_sem=sem["rr%d" % t], srcs=srcs, dsts=[near, near], alu_op=MAX))
-                sent[0] += 8
-            g.remote_dma_fused(trs, local_sem=sem.snt)
-
-    q = [i for i, p in enumerate(PAIR) if k in p][0]
-    j = PAIR[q].index(k)
-    partner = PAIR[q][1 - j]
-    others = [(k + 1 + i) % 8 for i in range(7)]
     for t in range(S):
-        mine, his = 8 * t + 2 * q + j, 8 * t + 2 * q + 1 - j
-        g.wait_ge(sem["rr%d" % t], 16)
+        g.wait_ge(sem["sc%d" % t], 14)
+        srcs = [T.land[7 * t + i] for i in range(7)] + [T.xs[8 * t + mine]]
+        g.remote_dma_fused([RemoteDMATransfer(dst_ids=[did(helper(mine))], dma_engine_mask=0xFF,
+                                              remote_sem=sem["hp%d" % t], srcs=srcs, dsts=[T.land[2 * t + side]],
+                                              alu_op=MAX)], local_sem=sem.snt)
+        sent[0] += 8
+
+    for t in range(S):
+        g.wait_ge(sem["fr%d" % t], 8)
         trs = []
-        for lo, hi, mask in ((0, 4, 0x00FF), (4, 6, 0x0F00), (6, 7, 0x3000)):
-            ds = others[lo:hi]
-            trs.append(RemoteDMATransfer(dst_ids=[did(base + d) for d in ds], dma_engine_mask=mask,
-                                         remote_sem=sem["fa%d" % t], srcs=[T.rl[4 * t + j], T.rl[4 * t + 2 + j]],
-                                         dsts=[T.fin[mine] for d in ds], alu_op=MAX))
-        trs.append(RemoteDMATransfer(dst_ids=[did(base + partner)], dma_engine_mask=0xC000, remote_sem=sem["fa%d" % t],
-                                     srcs=[T.rl[4 * t + 1 - j], T.rl[4 * t + 3 - j]], dsts=[T.fin[his]], alu_op=MAX))
-        sent[0] += 16
+        for i, d in enumerate(others):
+            trs.append(RemoteDMATransfer(dst_ids=[did(base + d)], dma_engine_mask=3 << (2 + 2 * i),
+                                         remote_sem=sem["ag%d" % t], src=T.fin[8 * t + mine], dst=T.fin[8 * t + mine],
+                                         alu_op=0))
+            sent[0] += 2
         g.remote_dma_fused(trs, local_sem=sem.snt)
 
     for t in range(S):
-        g.sync.wait_ge(sem["fa%d" % t], 4 * 8 + 2 * 4 + 2 + 2)
+        g.sync.wait_ge(sem["fr%d" % t], 8)
+        g.sync.wait_ge(sem["ag%d" % t], 14)
         g.sync.dma_start(T.y[R * t:R * t + R, :], T.fin[8 * t:8 * t + 8]).then_inc(sem.st, 16)
     g.sync.wait_ge(sem.st, 16 * S)
     g.wait_ge(sem.snt, sent[0])

from concourse.bass import DstId, RemoteDMATransfer

S = 2
W = 256 // S
SCRATCH = {
    "xs": ("dram", [8 * S, 128, W], "bfloat16"),
    "land": ("dram", [7 * S, 128, W], "bfloat16"),
    "fin": ("dram", [8 * S, 128, W], "bfloat16"),
}
SEMAPHORES = ["snt", "st"] + ["%s%d" % (n, t) for n in ("ld", "sc", "hp", "fr", "ag") for t in range(S)]
MAX = 2


def rank_program(g, core, T, topo):
    sem = T.sem
    bases = (T.cores[0], T.cores[8])
    R = 128 // S
    sent = [0]

    def did(dst):
        rid, pid = topo.addr(dst, core)
        return DstId(rid=rid, pnc=pid)

    def owner(e, side):
        return bases[side] + (e ^ 2 if side else e)

    def helper(e):
        return (bases[0] ^ 8) + e if e & 2 else (bases[1] ^ 8) + (e | 2)

    if T.rank_of(core) is None:
        for e in range(8):
            if helper(e) == core:
                for t in range(S):
                    g.wait_ge(sem["hp%d" % t], 16)
                    g.remote_dma_fused([RemoteDMATransfer(
                        dst_ids=[did(owner(e, 0)), did(owner(e, 1))], dma_engine_mask=0xFF, remote_sem=sem["fr%d" % t],
                        srcs=[T.land[2 * t], T.land[2 * t + 1]], dsts=[T.fin[8 * t + e], T.fin[8 * t + e]],
                        alu_op=MAX)], local_sem=sem.snt)
                g.wait_ge(sem.snt, 8 * S)
        return

    k = core % 8
    base = core - k
    side = bases.index(base)
    mine = k ^ 2 if side else k
    others = [d for d in range(8) if d != k]

    for t in range(S):
        g.sync.dma_start(T.xs[8 * t:8 * t + 8], T.x[R * t:R * t + R, :]).then_inc(sem["ld%d" % t], 16)

    for t in range(S):
        g.wait_ge(sem["ld%d" % t], 16)
        trs = []
        for i, d in enumerate(others):
            e = d ^ 2 if side else d
            idx = k if k < d else k - 1
            trs.append(RemoteDMATransfer(dst_ids=[did(base + d)], dma_engine_mask=3 << (2 + 2 * i),
                                         remote_sem=sem["sc%d" % t], src=T.xs[8 * t + e], dst=T.land[7 * t + idx],
                                         alu_op=0))
            sent[0] += 2
        g.remote_dma_fused(trs, local_sem=sem.snt)

    for t in range(S):
        g.wait_ge(sem["sc%d" % t], 14)
        srcs = [T.land[7 * t + i] for i in range(7)] + [T.xs[8 * t + mine]]
        g.remote_dma_fused([RemoteDMATransfer(dst_ids=[did(helper(mine))], dma_engine_mask=0xFF,
                                              remote_sem=sem["hp%d" % t], srcs=srcs, dsts=[T.land[2 * t + side]],
                                              alu_op=MAX)], local_sem=sem.snt)
        sent[0] += 8

    for t in range(S):
        g.wait_ge(sem["fr%d" % t], 8)
        trs = []
        for i, d in enumerate(others):
            trs.append(RemoteDMATransfer(dst_ids=[did(base + d)], dma_engine_mask=3 << (2 + 2 * i),
                                         remote_sem=sem["ag%d" % t], src=T.fin[8 * t + mine], dst=T.fin[8 * t + mine],
                                         alu_op=0))
            sent[0] += 2
        g.remote_dma_fused(trs, local_sem=sem.snt)

    for t in range(S):
        g.sync.wait_ge(sem["fr%d" % t], 8)
        g.sync.wait_ge(sem["ag%d" % t], 14)
        g.sync.dma_start(T.y[R * t:R * t + R, :], T.fin[8 * t:8 * t + 8]).then_inc(sem.st, 16)
    g.sync.wait_ge(sem.st, 16 * S)
    g.wait_ge(sem.snt, sent[0])
